import numpy as np
import ml_dtypes


def mxq(x, axis, fmt="e4m3"):
    dtype, down = {"e4m3": (ml_dtypes.float8_e4m3fn, 7), "e5m2": (ml_dtypes.float8_e5m2, 14)}[fmt]
    v = np.moveaxis(np.asarray(x, np.float32).astype(ml_dtypes.bfloat16).astype(np.float64), axis, -1)
    blocks = v.reshape(v.shape[:-1] + (-1, 32))
    amax = np.abs(blocks).max(-1, keepdims=True)
    byte = np.maximum(np.where(amax > 0, np.frexp(amax)[1] - 1 + 127, 0) - down, 1)
    scale = np.exp2(byte - 127.0)
    codes = (blocks / scale).astype(np.float32).astype(dtype).astype(np.float64)
    return np.moveaxis((codes * scale).reshape(v.shape), -1, axis)


WIDE = False


def mx_kscale(k):
    if not WIDE:
        return np.ones(k)
    levels = np.array([10, -10, 5, -5, 0])
    if k % 512:
        return np.exp2(np.random.permutation(np.resize(levels, k // 32))).repeat(32)
    a = np.empty((k // 512, 16))
    for p in range(k // 512):
        a[p, :8] = np.random.permutation(np.resize(levels, 8))
        for g in range(8):
            far = levels[np.abs(levels - a[p, g]) >= 10]
            a[p, g + 8] = far[np.random.randint(len(far))]
    return np.exp2(a.ravel()).repeat(32)


def f64(x):
    return np.asarray(x).astype(np.float64)


def striped(idx):
    return np.tile(idx.reshape(-1, 16).T, (8, 1)).astype(np.uint16)


def unstriped(offs):
    return offs[:16].T.reshape(-1).astype(np.int64)


def striped8(idx):
    return np.concatenate([x.reshape(-1, 16).T for x in idx]).astype(np.uint16)


def runs(offs, k):
    lists = np.stack([offs[16 * r : 16 * r + 16].T.reshape(-1) for r in range(8)]).astype(np.int64)
    return lists[np.arange(k) % 512 // 64]


def pack_weight(w):
    k, n = w.shape
    w = f64(np.asarray(w, np.float32).astype(ml_dtypes.bfloat16)).reshape(k // 32, 32, n)
    amax = np.abs(w).max(1)
    byte = np.clip(np.where(amax > 0, np.frexp(amax)[1] - 1 + 127 - 7, 1), 1, 254)
    scaled = (w * np.exp2(127.0 - byte)[:, None, :]).reshape(k, n).astype(np.float32)
    words = np.ascontiguousarray(scaled.reshape(k // 512, 128, 4, n).transpose(0, 1, 3, 2)).astype(ml_dtypes.float8_e4m3fn).view(np.uint8)
    return words, np.ascontiguousarray(byte.astype(np.uint8).reshape(k // 512, 16, n))


def unpack_weight(words, scales):
    g, p, n, _ = words.shape
    vals = np.ascontiguousarray(words).view(ml_dtypes.float8_e4m3fn).astype(np.float64) * np.repeat(np.exp2(scales.astype(np.float64) - 127.0), 8, axis=1)[..., None]
    return vals.transpose(0, 1, 3, 2).reshape(g * 512, n)


K, T, S, N, H, U = 512, 2048, 512, 512, 512, 1024


def setup_inputs():
    n = np.random.standard_normal
    s = mx_kscale(K)[:, None]
    u = mx_kscale(S)
    packed_xT = pack_weight(n((K, T)) * s)
    return {
        "x_words": packed_xT[0],
        "x_scales": packed_xT[1],
        "wa": (n((K, H)) / np.sqrt(K) / s).astype(np.float32),
        "gt": (np.random.uniform(0.5, 1.5, (S, 1)) * u[:, None]).astype(np.float32),
        "w1": (n((S, N)) / np.sqrt(S) / u[:, None]).astype(np.float32),
        "mem": n((N, U)).astype(np.float32),
        "offs": striped(np.random.permutation(T)[:S]),
        "n1": striped8(np.stack([np.random.permutation(H) for _ in range(8)])),
        "n2": striped8(np.stack([np.random.permutation(H) for _ in range(8)])),
        "n3": striped8(np.stack([np.random.permutation(U)[:H] for _ in range(8)])),
    }


def reference(x_words, x_scales, wa, gt, w1, mem, offs, n1, n2, n3):
    xq = unpack_weight(x_words, x_scales)[:, unstriped(offs)]
    y = xq.T @ mxq(f64(wa), 0, "e4m3")
    st = y - (y[np.arange(S)[:, None], runs(n1, S)])
    z = f64(gt) * (st / (np.abs(st[np.arange(S)[:, None], runs(n2, S)]) + 0.5))
    h = mxq(f64(w1), 0, "e4m3").T @ mxq(z, 0, "e4m3")
    nw = np.maximum(h, 0.5 * (f64(mem)[np.arange(N)[:, None], runs(n3, N)]))
    out = f64(mem).copy()
    out[np.arange(N)[:, None], runs(n3, N)] = nw
    return out

@@ -1,0 +1,209 @@
+from contextlib import ExitStack
+
+import concourse.mybir as mybir
+
+K, T, S, N, H, U = 512, 2048, 512, 512, 512, 1024
+FLOPS = 2 * K * S * H + 2 * S * N * H
+
+F32 = mybir.dt.float32
+BF16 = mybir.dt.bfloat16
+I32 = mybir.dt.int32
+U32 = mybir.dt.uint32
+U16 = mybir.dt.uint16
+U8 = mybir.dt.uint8
+FP8X4 = mybir.dt.float8_e4m3fn_x4
+ALU = mybir.AluOpType
+ACT = mybir.ActivationFunctionType
+
+P = 128
+R = 4
+HALF = H // 2
+
+
+def tile_picked_tokhopnpagex_none_p_kernel(tc, x_words, x_scales, wa, gt, w1, mem, offs, n1, n2, n3, out):
+    nc = tc.nc
+
+    def gather(on_vector, dst, window, offsets):
+        if on_vector:
+            nc.vector.tensor_copy(out=dst, in_=window.indirect(offsets))
+        else:
+            nc.scalar.activation(out=dst, in_=window.indirect(offsets), func=ACT.Copy)
+
+    def entries(lists, s):
+        return lists[:, s * HALF // 16 : (s + 1) * HALF // 16]
+
+    def cols(s):
+        return slice(s * HALF, (s + 1) * HALF)
+
+    with ExitStack() as ctx:
+        keep = ctx.enter_context(tc.tile_pool(name="keep", bufs=1))
+        psum = ctx.enter_context(tc.psum_pool(name="psum", bufs=1))
+
+        def sbuf(shape, dtype, name, tag=None):
+            return keep.tile(shape, dtype, name=name, tag=tag or name, align_bytes=64)
+
+        offs_sb = sbuf([P, S // 16], U16, "offs_sb")
+        n1_sb = sbuf([P, H // 16], U16, "n1_sb")
+        n2_sb = sbuf([P, H // 16], U16, "n2_sb")
+        n3_sb = sbuf([P, H // 16], U16, "n3_sb")
+        xw = sbuf([P, T], I32, "xw")
+        xs = sbuf([P, T], U8, "xs")
+        gt_sb = sbuf([P, R], F32, "gt_sb")
+        wa_raw = [sbuf([P, R, HALF], F32, f"wa_raw{b}") for b in range(2)]
+        w1_raw = sbuf([P, R, N], F32, "w1_raw")
+        page = [sbuf([P, U], F32, f"page{u}") for u in range(R)]
+
+        nc.vector.memset(xs[:].bitcast(I32), 0)
+        wa_rows = wa.rearrange("(p t) j -> p t j", t=R)
+        nc.sync.dma_start(out=wa_raw[0][:], in_=wa_rows[:, :, cols(0)])
+        for q in range(4):
+            nc.sync.dma_start(out=xs[32 * q : 32 * q + 4, :].bitcast(I32), in_=x_scales[0, 4 * q : 4 * q + 4, :].bitcast(I32))
+        nc.sync.dma_start(offs_sb[:], offs)
+        nc.sync.dma_start(out=wa_raw[1][:], in_=wa_rows[:, :, cols(1)])
+        nc.sync.dma_start(out=xw[:], in_=x_words[0].rearrange("p n t -> p (n t)").bitcast(I32))
+        nc.sync.dma_start(n1_sb[:], n1)
+        nc.sync.dma_start(out=w1_raw[:], in_=w1.rearrange("(p t) m -> p t m", t=R))
+        nc.sync.dma_start(n2_sb[:], n2)
+        nc.sync.dma_start(n3_sb[:], n3)
+        nc.sync.dma_start(out=gt_sb[:], in_=gt.rearrange("(p t) o -> p (t o)", t=R))
+        mem_rows = mem.rearrange("(p u) w -> p u w", u=R)
+        out_rows = out.rearrange("(p u) w -> p u w", u=R)
+        for u in range(R):
+            nc.sync.dma_start(out=page[u][:], in_=mem_rows[:, u, :])
+
+        xq = sbuf([P, S], U32, "xq")
+        xq_s = sbuf([P, S], U8, "xq_s")
+        nc.vector.tensor_copy(out=xq_s[:].rearrange("p (t c) -> p c t", t=R), in_=xs[:].indirect(offs_sb[:]))
+
+        wa_q = sbuf([P, H], U32, "wa_q")
+        wa_s = sbuf([P, H], U8, "wa_s")
+        wa_bf = sbuf([P, H * R], BF16, "wa_bf")
+        for b in range(2):
+            nc.scalar.copy(
+                out=wa_bf[:, b * HALF * R : (b + 1) * HALF * R].rearrange("p (c i t) -> p c t i", i=4, t=R),
+                in_=wa_raw[b][:].rearrange("p t (c i) -> p c t i", i=4),
+            )
+        nc.vector.quantize_mx(out=wa_q[:].bitcast(FP8X4), scales=wa_s[:], in_=wa_bf[:])
+        nc.vector.tensor_copy(out=xq[:].rearrange("p (t c) -> p c t", t=R), in_=xw[:].bitcast(U32).indirect(offs_sb[:]))
+
+        y_ps = [psum.tile([P, H], F32, name=f"y_ps{t}") for t in range(R)]
+        for t in range(R):
+            nc.tensor.matmul_mx(
+                out=y_ps[t][:],
+                lhsT=xq[:, t * P : (t + 1) * P].bitcast(FP8X4),
+                lhsT_scale=xq_s[:, t * P : (t + 1) * P],
+                rhs=wa_q[:].bitcast(FP8X4),
+                rhs_scale=wa_s[:],
+                start=True,
+                stop=True,
+            )
+
+        y_sb = [sbuf([P, H], F32, f"y_sb{t}") for t in range(R)]
+        y_far = [sbuf([P, 2, H], F32, f"y_far{g}") for g in range(2)]
+        st = [sbuf([P, H], F32, f"st{t}") for t in range(R)]
+        for t in range(R):
+            nc.scalar.copy(out=y_sb[t][:], in_=y_ps[t][:])
+        for t in range(R):
+            for s in range(2):
+                gather(t < 2, y_far[t // 2][:, t % 2, cols(s)], y_sb[t][:], entries(n1_sb, s))
+        for t in range(R):
+            nc.vector.tensor_tensor(out=st[t][:], in0=y_ps[t][:], in1=y_far[t // 2][:, t % 2, :], op=ALU.subtract)
+
+        def denominators(s, far, size, sq, inv, groups, on_vector):
+            for t in range(R):
+                gather(t in on_vector, far[:, t, :], st[t][:], entries(n2_sb, s))
+            for g in groups:
+                nc.scalar.activation(out=size[:, g, :], in_=far[:, g, :], func=ACT.Abs)
+            for g in groups:
+                nc.scalar.activation(out=sq[:, g, :], in_=size[:, g, :], func=ACT.Square, bias=0.5)
+            for g in groups:
+                nc.scalar.activation(out=inv[:, g, :], in_=sq[:, g, :], func=ACT.Abs_reciprocal_sqrt)
+
+        def numerators(s, inv):
+            z_bf = sbuf([P, R, HALF], BF16, f"z_bf{s}")
+            for t in range(R):
+                nc.vector.scalar_tensor_tensor(
+                    out=z_bf[:, t, :], in0=inv[:, t, :], scalar=gt_sb[:, t : t + 1], in1=st[t][:, cols(s)], op0=ALU.mult, op1=ALU.mult
+                )
+            return z_bf
+
+        def weave(s, z_bf, copy):
+            z_wv = sbuf([P, HALF * R], BF16, f"z_wv{s}")
+            copy(out=z_wv[:].rearrange("p (c i t) -> p c t i", i=4, t=R), in_=z_bf[:].rearrange("p t (c i) -> p c t i", i=4))
+            return z_wv
+
+        def second_product(s, z_wv):
+            z_q = sbuf([P, HALF], U32, f"z_q{s}")
+            z_s = sbuf([P, HALF], U8, f"z_s{s}")
+            nc.vector.quantize_mx(out=z_q[:].bitcast(FP8X4), scales=z_s[:], in_=z_wv[:])
+            banks = [psum.tile([P, 2, HALF], F32, name=f"h_ps{s}_{b}") for b in range(2)]
+            for u in range(R):
+                nc.tensor.matmul_mx(
+                    out=banks[u // 2][:, u % 2, :],
+                    lhsT=w1_q[:, u * P : (u + 1) * P].bitcast(FP8X4),
+                    lhsT_scale=w1_s[:, u * P : (u + 1) * P],
+                    rhs=z_q[:].bitcast(FP8X4),
+                    rhs_scale=z_s[:],
+                    start=True,
+                    stop=True,
+                )
+            return banks
+
+        def larger(s, banks, u, count, old_cols, new):
+            nc.vector.scalar_tensor_tensor(
+                out=new[:], in0=old_cols, scalar=0.5, in1=banks[u // 2][:, u % 2 : u % 2 + count, :], op0=ALU.mult, op1=ALU.max
+            )
+
+        def scatter(s, u, new_cols):
+            nc.vector.tensor_copy(out=page[u][:].indirect(entries(n3_sb, s)), in_=new_cols)
+            if s == 1:
+                nc.sync.dma_start(out=out_rows[:, u, :], in_=page[u][:])
+
+        far0, size0, sq0, inv0 = [sbuf([P, R, HALF], F32, name) for name in ("far0", "size0", "sq0", "inv0")]
+        denominators(0, far0, size0, sq0, inv0, [slice(0, 2), slice(2, 4)], [2, 3])
+
+        w1_bf = sbuf([P, N * R], BF16, "w1_bf", "y_far1")
+        w1_q = sbuf([P, N], U32, "w1_q")
+        w1_s = sbuf([P, N], U8, "w1_s")
+        nc.vector.tensor_copy(out=w1_bf[:].rearrange("p (u m t) -> p m u t", u=R, t=R), in_=w1_raw[:].rearrange("p t (m u) -> p m u t", u=R))
+        nc.vector.quantize_mx(out=w1_q[:].bitcast(FP8X4), scales=w1_s[:], in_=w1_bf[:])
+
+        banks0 = second_product(0, weave(0, numerators(0, inv0), nc.vector.tensor_copy))
+
+        old0 = sbuf([P, 1, H], F32, "old0", "z_wv0")
+        old1 = sbuf([P, 1, H], F32, "old1", "sq0")
+        gather(True, old0[:, 0, :], page[0][:], n3_sb[:])
+        gather(False, old1[:, 0, :], page[1][:], n3_sb[:])
+
+        far1 = sbuf([P, R, HALF], F32, "far1", "size0")
+        size1, sq1, inv1 = [sbuf([P, R, HALF], F32, name) for name in ("size1", "sq1", "inv1")]
+        denominators(1, far1, size1, sq1, inv1, [slice(0, 4)], [])
+
+        new = [sbuf([P, 1, HALF], F32, f"new0{u}") for u in range(2)]
+        larger(0, banks0, 0, 1, old0[:, :, cols(0)], new[0])
+        larger(0, banks0, 1, 1, old1[:, :, cols(0)], new[1])
+        scatter(0, 0, new[0][:, 0, :])
+        scatter(0, 1, new[1][:, 0, :])
+
+        old23 = sbuf([P, 2, H], F32, "old23", "sq1")
+        for k in range(2):
+            gather(False, old23[:, k, :], page[2 + k][:], n3_sb[:])
+
+        z_bf1 = numerators(1, inv1)
+        new02 = sbuf([P, 1, HALF], F32, "new02", "inv1")
+        larger(0, banks0, 2, 1, old23[:, 0:1, cols(0)], new02)
+        scatter(0, 2, new02[:, 0, :])
+        banks1 = second_product(1, weave(1, z_bf1, nc.scalar.copy))
+        new03 = sbuf([P, 1, HALF], F32, "new03", "z_wv1")
+        larger(0, banks0, 3, 1, old23[:, 1:2, cols(0)], new03)
+        scatter(0, 3, new03[:, 0, :])
+
+        new = [sbuf([P, 1, HALF], F32, f"new1{u}") for u in range(2)]
+        new12 = sbuf([P, 2, HALF], F32, "new12")
+        larger(1, banks1, 0, 1, old0[:, :, cols(1)], new[0])
+        larger(1, banks1, 1, 1, old1[:, :, cols(1)], new[1])
+        scatter(1, 0, new[0][:, 0, :])
+        scatter(1, 1, new[1][:, 0, :])
+        larger(1, banks1, 2, 2, old23[:, :, cols(1)], new12)
+        scatter(1, 2, new12[:, 0, :])
+        scatter(1, 3, new12[:, 1, :])

@@ -53,6 +53,11 @@ def tile_picked_tokhopnpagex_none_p_kernel(tc, x_words, x_scales, wa, gt, w1, me
         w1_raw = sbuf([P, R, N], F32, "w1_raw")
         page = [sbuf([P, U], F32, f"page{u}") for u in range(R)]
 
+        warm_in = sbuf([P, 8], F32, "warm_in")
+        warm_out = sbuf([P, 8], F32, "warm_out")
+        nc.gpsimd.memset(warm_in[:], 1.0)
+        nc.scalar.activation(out=warm_out[:], in_=warm_in[:], func=ACT.Abs_reciprocal_sqrt)
+
         nc.vector.memset(xs[:].bitcast(I32), 0)
         wa_rows = wa.rearrange("(p t) j -> p t j", t=R)
         nc.sync.dma_start(out=wa_raw[0][:], in_=wa_rows[:, :, cols(0)])

@@ -18,22 +18,46 @@ ACT = mybir.ActivationFunctionType
 P = 128
 R = 4
 HALF = H // 2
+LINE = 4
+WA_ON_SCALAR = 192
+TILES_ON_VECTOR = 2
 
 
 def tile_picked_tokhopnpagex_none_p_kernel(tc, x_words, x_scales, wa, gt, w1, mem, offs, n1, n2, n3, out):
     nc = tc.nc
 
-    def gather(on_vector, dst, window, offsets):
-        if on_vector:
-            nc.vector.tensor_copy(out=dst, in_=window.indirect(offsets))
-        else:
-            nc.scalar.activation(out=dst, in_=window.indirect(offsets), func=ACT.Copy)
+    def gather_on_vector(dst, window, offsets):
+        nc.vector.tensor_copy(out=dst, in_=window.indirect(offsets))
 
-    def entries(lists, s):
-        return lists[:, s * HALF // 16 : (s + 1) * HALF // 16]
+    def gather_on_scalar(dst, window, offsets):
+        nc.scalar.activation(out=dst, in_=window.indirect(offsets), func=ACT.Copy)
 
-    def cols(s):
-        return slice(s * HALF, (s + 1) * HALF)
+    def abs_on_vector(dst, src):
+        nc.vector.scalar_tensor_tensor(out=dst, in0=src, scalar=-1.0, in1=src, op0=ALU.mult, op1=ALU.max)
+
+    def abs_on_scalar(dst, src):
+        nc.scalar.activation(out=dst, in_=src, func=ACT.Abs)
+
+    def entries(lists, half):
+        return lists[:, half * HALF // 16 : (half + 1) * HALF // 16]
+
+    def cols(half):
+        return slice(half * HALF, (half + 1) * HALF)
+
+    def interleave(copy, dst, src):
+        copy(out=dst.rearrange("p (c i t) -> p c t i", i=LINE, t=R), in_=src.rearrange("p t (c i) -> p c t i", i=LINE))
+
+    def product(dst, lhs_codes, lhs_scales, block, rhs_codes, rhs_scales):
+        rows = slice(block * P, (block + 1) * P)
+        nc.tensor.matmul_mx(
+            out=dst,
+            lhsT=lhs_codes[:, rows].bitcast(FP8X4),
+            lhsT_scale=lhs_scales[:, rows],
+            rhs=rhs_codes[:].bitcast(FP8X4),
+            rhs_scale=rhs_scales[:],
+            start=True,
+            stop=True,
+        )
 
     with ExitStack() as ctx:
         keep = ctx.enter_context(tc.tile_pool(name="keep", bufs=1))
@@ -42,173 +66,145 @@ def tile_picked_tokhopnpagex_none_p_kernel(tc, x_words, x_scales, wa, gt, w1, me
         def sbuf(shape, dtype, name, tag=None):
             return keep.tile(shape, dtype, name=name, tag=tag or name, align_bytes=64)
 
-        offs_sb = sbuf([P, S // 16], U16, "offs_sb")
-        n1_sb = sbuf([P, H // 16], U16, "n1_sb")
-        n2_sb = sbuf([P, H // 16], U16, "n2_sb")
-        n3_sb = sbuf([P, H // 16], U16, "n3_sb")
-        xw = sbuf([P, T], I32, "xw")
-        xs = sbuf([P, T], U8, "xs")
-        gt_sb = sbuf([P, R], F32, "gt_sb")
-        wa_raw = [sbuf([P, R, HALF], F32, f"wa_raw{b}") for b in range(2)]
-        w1_raw = sbuf([P, R, N], F32, "w1_raw")
-        page = [sbuf([P, U], F32, f"page{u}") for u in range(R)]
-
         warm_in = sbuf([P, 8], F32, "warm_in")
         warm_out = sbuf([P, 8], F32, "warm_out")
         nc.gpsimd.memset(warm_in[:], 1.0)
         nc.scalar.activation(out=warm_out[:], in_=warm_in[:], func=ACT.Abs_reciprocal_sqrt)
 
-        nc.vector.memset(xs[:].bitcast(I32), 0)
-        wa_rows = wa.rearrange("(p t) j -> p t j", t=R)
-        nc.sync.dma_start(out=wa_raw[0][:], in_=wa_rows[:, :, cols(0)])
-        for q in range(4):
-            nc.sync.dma_start(out=xs[32 * q : 32 * q + 4, :].bitcast(I32), in_=x_scales[0, 4 * q : 4 * q + 4, :].bitcast(I32))
+        offs_sb = sbuf([P, S // 16], U16, "offs_sb")
+        n1_sb = sbuf([P, H // 16], U16, "n1_sb")
+        n2_sb = sbuf([P, H // 16], U16, "n2_sb")
+        n3_sb = sbuf([P, H // 16], U16, "n3_sb")
+        x_table = sbuf([P, T], I32, "x_table")
+        x_table_scales = sbuf([P, T], U8, "x_table_scales")
+        gt_sb = sbuf([P, R], F32, "gt_sb")
+        wa_raw = sbuf([P, R, H], F32, "wa_raw")
+        w1_raw = sbuf([P, R, N], F32, "w1_raw")
+        page = [sbuf([P, U], F32, f"page{u}") for u in range(R)]
+        mem_rows = mem.rearrange("(p u) w -> p u w", u=R)
+        out_rows = out.rearrange("(p u) w -> p u w", u=R)
+
+        nc.vector.memset(x_table_scales[:].bitcast(I32), 0)
+        nc.sync.dma_start(out=wa_raw[:], in_=wa.rearrange("(p t) j -> p t j", t=R))
         nc.sync.dma_start(offs_sb[:], offs)
-        nc.sync.dma_start(out=wa_raw[1][:], in_=wa_rows[:, :, cols(1)])
-        nc.sync.dma_start(out=xw[:], in_=x_words[0].rearrange("p n t -> p (n t)").bitcast(I32))
+        for q in (0, 2, 1, 3):
+            nc.sync.dma_start(out=x_table_scales[32 * q : 32 * q + 4, :].bitcast(I32), in_=x_scales[0, 4 * q : 4 * q + 4, :].bitcast(I32))
+        nc.sync.dma_start(out=x_table[:], in_=x_words[0].rearrange("p n t -> p (n t)").bitcast(I32))
         nc.sync.dma_start(n1_sb[:], n1)
         nc.sync.dma_start(out=w1_raw[:], in_=w1.rearrange("(p t) m -> p t m", t=R))
         nc.sync.dma_start(n2_sb[:], n2)
         nc.sync.dma_start(n3_sb[:], n3)
         nc.sync.dma_start(out=gt_sb[:], in_=gt.rearrange("(p t) o -> p (t o)", t=R))
-        mem_rows = mem.rearrange("(p u) w -> p u w", u=R)
-        out_rows = out.rearrange("(p u) w -> p u w", u=R)
         for u in range(R):
             nc.sync.dma_start(out=page[u][:], in_=mem_rows[:, u, :])
 
-        xq = sbuf([P, S], U32, "xq")
-        xq_s = sbuf([P, S], U8, "xq_s")
-        nc.vector.tensor_copy(out=xq_s[:].rearrange("p (t c) -> p c t", t=R), in_=xs[:].indirect(offs_sb[:]))
-
-        wa_q = sbuf([P, H], U32, "wa_q")
-        wa_s = sbuf([P, H], U8, "wa_s")
         wa_bf = sbuf([P, H * R], BF16, "wa_bf")
-        for b in range(2):
-            nc.scalar.copy(
-                out=wa_bf[:, b * HALF * R : (b + 1) * HALF * R].rearrange("p (c i t) -> p c t i", i=4, t=R),
-                in_=wa_raw[b][:].rearrange("p t (c i) -> p c t i", i=4),
-            )
-        nc.vector.quantize_mx(out=wa_q[:].bitcast(FP8X4), scales=wa_s[:], in_=wa_bf[:])
-        nc.vector.tensor_copy(out=xq[:].rearrange("p (t c) -> p c t", t=R), in_=xw[:].bitcast(U32).indirect(offs_sb[:]))
+        wa_codes = sbuf([P, H], U32, "wa_codes")
+        wa_scales = sbuf([P, H], U8, "wa_scales")
+        x_codes = sbuf([P, S], U32, "x_codes")
+        x_code_scales = sbuf([P, S], U8, "x_code_scales")
+        interleave(nc.scalar.copy, wa_bf[:, : WA_ON_SCALAR * R], wa_raw[:, :, :WA_ON_SCALAR])
+        interleave(nc.vector.tensor_copy, wa_bf[:, WA_ON_SCALAR * R :], wa_raw[:, :, WA_ON_SCALAR:])
+        gather_on_vector(x_code_scales[:].rearrange("p (t c) -> p c t", t=R), x_table_scales[:], offs_sb[:])
+        nc.vector.quantize_mx(out=wa_codes[:].bitcast(FP8X4), scales=wa_scales[:], in_=wa_bf[:])
+        gather_on_vector(x_codes[:].rearrange("p (t c) -> p c t", t=R), x_table[:].bitcast(U32), offs_sb[:])
 
         y_ps = [psum.tile([P, H], F32, name=f"y_ps{t}") for t in range(R)]
         for t in range(R):
-            nc.tensor.matmul_mx(
-                out=y_ps[t][:],
-                lhsT=xq[:, t * P : (t + 1) * P].bitcast(FP8X4),
-                lhsT_scale=xq_s[:, t * P : (t + 1) * P],
-                rhs=wa_q[:].bitcast(FP8X4),
-                rhs_scale=wa_s[:],
-                start=True,
-                stop=True,
-            )
+            product(y_ps[t][:], x_codes, x_code_scales, t, wa_codes, wa_scales)
+
+        w1_bf = sbuf([P, N * R], BF16, "w1_bf")
+        nc.vector.tensor_copy(out=w1_bf[:].rearrange("p (u c t) -> p c u t", u=R, t=R), in_=w1_raw[:].rearrange("p t (c u) -> p c u t", u=R))
 
         y_sb = [sbuf([P, H], F32, f"y_sb{t}") for t in range(R)]
-        y_far = [sbuf([P, 2, H], F32, f"y_far{g}") for g in range(2)]
-        st = [sbuf([P, H], F32, f"st{t}") for t in range(R)]
+        y_far_v = sbuf([P, TILES_ON_VECTOR, H], F32, "y_far_v", "w1_raw")
+        y_far_s = sbuf([P, R - TILES_ON_VECTOR, H], F32, "y_far_s")
+        y_far = [y_far_v[:, 0, :], y_far_v[:, 1, :], y_far_s[:, 0, :], y_far_s[:, 1, :]]
         for t in range(R):
             nc.scalar.copy(out=y_sb[t][:], in_=y_ps[t][:])
         for t in range(R):
-            for s in range(2):
-                gather(t < 2, y_far[t // 2][:, t % 2, cols(s)], y_sb[t][:], entries(n1_sb, s))
+            gather = gather_on_vector if t < TILES_ON_VECTOR else gather_on_scalar
+            for half in range(2):
+                gather(y_far[t][:, cols(half)], y_sb[t][:], entries(n1_sb, half))
+        st = [sbuf([P, H], F32, "st0"), sbuf([P, H], F32, "st1"), sbuf([P, H], F32, "st2", "y_sb1"), sbuf([P, H], F32, "st3", "y_sb0")]
         for t in range(R):
-            nc.vector.tensor_tensor(out=st[t][:], in0=y_ps[t][:], in1=y_far[t // 2][:, t % 2, :], op=ALU.subtract)
+            nc.vector.tensor_tensor(out=st[t][:], in0=y_ps[t][:], in1=y_far[t], op=ALU.subtract)
 
-        def denominators(s, far, size, sq, inv, groups, on_vector):
+        def reciprocals(half, st_far, gathers, groups):
+            size, square, inv = [sbuf([P, R, HALF], F32, f"{name}{half}") for name in ("size", "square", "inv")]
             for t in range(R):
-                gather(t in on_vector, far[:, t, :], st[t][:], entries(n2_sb, s))
-            for g in groups:
-                nc.scalar.activation(out=size[:, g, :], in_=far[:, g, :], func=ACT.Abs)
-            for g in groups:
-                nc.scalar.activation(out=sq[:, g, :], in_=size[:, g, :], func=ACT.Square, bias=0.5)
-            for g in groups:
-                nc.scalar.activation(out=inv[:, g, :], in_=sq[:, g, :], func=ACT.Abs_reciprocal_sqrt)
+                gathers[t](st_far[:, t, :], st[t][:], entries(n2_sb, half))
+            for tiles, absolute in groups:
+                absolute(size[:, tiles, :], st_far[:, tiles, :])
+                nc.scalar.activation(out=square[:, tiles, :], in_=size[:, tiles, :], func=ACT.Square, bias=0.5)
+                nc.scalar.activation(out=inv[:, tiles, :], in_=square[:, tiles, :], func=ACT.Abs_reciprocal_sqrt)
+            return inv
 
-        def numerators(s, inv):
-            z_bf = sbuf([P, R, HALF], BF16, f"z_bf{s}")
+        def make_z(half, inv, copy):
+            z_bf = sbuf([P, R, HALF], BF16, f"z_bf{half}")
+            z_woven = sbuf([P, HALF * R], BF16, f"z_woven{half}")
             for t in range(R):
                 nc.vector.scalar_tensor_tensor(
-                    out=z_bf[:, t, :], in0=inv[:, t, :], scalar=gt_sb[:, t : t + 1], in1=st[t][:, cols(s)], op0=ALU.mult, op1=ALU.mult
+                    out=z_bf[:, t, :], in0=inv[:, t, :], scalar=gt_sb[:, t : t + 1], in1=st[t][:, cols(half)], op0=ALU.mult, op1=ALU.mult
                 )
-            return z_bf
+            interleave(copy, z_woven[:], z_bf[:])
+            return z_woven
 
-        def weave(s, z_bf, copy):
-            z_wv = sbuf([P, HALF * R], BF16, f"z_wv{s}")
-            copy(out=z_wv[:].rearrange("p (c i t) -> p c t i", i=4, t=R), in_=z_bf[:].rearrange("p t (c i) -> p c t i", i=4))
-            return z_wv
-
-        def second_product(s, z_wv):
-            z_q = sbuf([P, HALF], U32, f"z_q{s}")
-            z_s = sbuf([P, HALF], U8, f"z_s{s}")
-            nc.vector.quantize_mx(out=z_q[:].bitcast(FP8X4), scales=z_s[:], in_=z_wv[:])
-            banks = [psum.tile([P, 2, HALF], F32, name=f"h_ps{s}_{b}") for b in range(2)]
+        def second_product(half, z_woven):
+            z_codes = sbuf([P, HALF], U32, f"z_codes{half}")
+            z_scales = sbuf([P, HALF], U8, f"z_scales{half}")
+            nc.vector.quantize_mx(out=z_codes[:].bitcast(FP8X4), scales=z_scales[:], in_=z_woven[:])
+            banks = [psum.tile([P, 2, HALF], F32, name=f"h_ps{half}_{b}") for b in range(2)]
+            h = [banks[u // 2][:, u % 2, :] for u in range(R)]
             for u in range(R):
-                nc.tensor.matmul_mx(
-                    out=banks[u // 2][:, u % 2, :],
-                    lhsT=w1_q[:, u * P : (u + 1) * P].bitcast(FP8X4),
-                    lhsT_scale=w1_s[:, u * P : (u + 1) * P],
-                    rhs=z_q[:].bitcast(FP8X4),
-                    rhs_scale=z_s[:],
-                    start=True,
-                    stop=True,
-                )
-            return banks
+                product(h[u], w1_codes, w1_scales, u, z_codes, z_scales)
+            return h
 
-        def larger(s, banks, u, count, old_cols, new):
-            nc.vector.scalar_tensor_tensor(
-                out=new[:], in0=old_cols, scalar=0.5, in1=banks[u // 2][:, u % 2 : u % 2 + count, :], op0=ALU.mult, op1=ALU.max
-            )
+        def fetch_old(u, gather, tag):
+            old = sbuf([P, H], F32, f"old{u}", tag)
+            gather(old[:], page[u][:], n3_sb[:])
+            return old
 
-        def scatter(s, u, new_cols):
-            nc.vector.tensor_copy(out=page[u][:].indirect(entries(n3_sb, s)), in_=new_cols)
-            if s == 1:
-                nc.sync.dma_start(out=out_rows[:, u, :], in_=page[u][:])
+        def larger(half, u, h, old, tag=None):
+            nw = sbuf([P, HALF], F32, f"nw{half}_{u}", tag)
+            nc.vector.scalar_tensor_tensor(out=nw[:], in0=old[:, cols(half)], scalar=0.5, in1=h[u], op0=ALU.mult, op1=ALU.max)
+            return nw
 
-        far0, size0, sq0, inv0 = [sbuf([P, R, HALF], F32, name) for name in ("far0", "size0", "sq0", "inv0")]
-        denominators(0, far0, size0, sq0, inv0, [slice(0, 2), slice(2, 4)], [2, 3])
+        def scatter(half, u, nw):
+            nc.vector.tensor_copy(out=page[u][:].indirect(entries(n3_sb, half)), in_=nw[:])
 
-        w1_bf = sbuf([P, N * R], BF16, "w1_bf", "y_far1")
-        w1_q = sbuf([P, N], U32, "w1_q")
-        w1_s = sbuf([P, N], U8, "w1_s")
-        nc.vector.tensor_copy(out=w1_bf[:].rearrange("p (u m t) -> p m u t", u=R, t=R), in_=w1_raw[:].rearrange("p t (m u) -> p m u t", u=R))
-        nc.vector.quantize_mx(out=w1_q[:].bitcast(FP8X4), scales=w1_s[:], in_=w1_bf[:])
+        inv0 = reciprocals(
+            0,
+            sbuf([P, R, HALF], F32, "st_far0"),
+            [gather_on_scalar, gather_on_scalar, gather_on_vector, gather_on_vector],
+            [(slice(0, 2), abs_on_scalar), (slice(2, 3), abs_on_scalar), (slice(3, 4), abs_on_vector)],
+        )
+        w1_codes = sbuf([P, N], U32, "w1_codes", "y_far_s")
+        w1_scales = sbuf([P, N], U8, "w1_scales")
+        nc.vector.quantize_mx(out=w1_codes[:].bitcast(FP8X4), scales=w1_scales[:], in_=w1_bf[:])
+        h0 = second_product(0, make_z(0, inv0, nc.vector.tensor_copy))
+        old0 = fetch_old(0, gather_on_vector, "z_woven0")
+        old1 = fetch_old(1, gather_on_scalar, "square0")
 
-        banks0 = second_product(0, weave(0, numerators(0, inv0), nc.vector.tensor_copy))
+        inv1 = reciprocals(
+            1,
+            sbuf([P, R, HALF], F32, "st_far1", "size0"),
+            [gather_on_scalar] * R,
+            [(slice(0, 2), abs_on_scalar), (slice(2, 4), abs_on_scalar)],
+        )
+        nw01 = larger(0, 1, h0, old1)
+        nw00 = larger(0, 0, h0, old0)
+        scatter(0, 1, nw01)
+        scatter(0, 0, nw00)
 
-        old0 = sbuf([P, 1, H], F32, "old0", "z_wv0")
-        old1 = sbuf([P, 1, H], F32, "old1", "sq0")
-        gather(True, old0[:, 0, :], page[0][:], n3_sb[:])
-        gather(False, old1[:, 0, :], page[1][:], n3_sb[:])
+        old2 = fetch_old(2, gather_on_scalar, "square1")
+        z_woven1 = make_z(1, inv1, nc.scalar.copy)
+        old3 = fetch_old(3, gather_on_scalar, "z_bf1")
+        scatter(0, 2, larger(0, 2, h0, old2))
+        h1 = second_product(1, z_woven1)
+        scatter(0, 3, larger(0, 3, h0, old3, "z_woven1"))
 
-        far1 = sbuf([P, R, HALF], F32, "far1", "size0")
-        size1, sq1, inv1 = [sbuf([P, R, HALF], F32, name) for name in ("size1", "sq1", "inv1")]
-        denominators(1, far1, size1, sq1, inv1, [slice(0, 4)], [])
-
-        new = [sbuf([P, 1, HALF], F32, f"new0{u}") for u in range(2)]
-        larger(0, banks0, 0, 1, old0[:, :, cols(0)], new[0])
-        larger(0, banks0, 1, 1, old1[:, :, cols(0)], new[1])
-        scatter(0, 0, new[0][:, 0, :])
-        scatter(0, 1, new[1][:, 0, :])
-
-        old23 = sbuf([P, 2, H], F32, "old23", "sq1")
-        for k in range(2):
-            gather(False, old23[:, k, :], page[2 + k][:], n3_sb[:])
-
-        z_bf1 = numerators(1, inv1)
-        new02 = sbuf([P, 1, HALF], F32, "new02", "inv1")
-        larger(0, banks0, 2, 1, old23[:, 0:1, cols(0)], new02)
-        scatter(0, 2, new02[:, 0, :])
-        banks1 = second_product(1, weave(1, z_bf1, nc.scalar.copy))
-        new03 = sbuf([P, 1, HALF], F32, "new03", "z_wv1")
-        larger(0, banks0, 3, 1, old23[:, 1:2, cols(0)], new03)
-        scatter(0, 3, new03[:, 0, :])
-
-        new = [sbuf([P, 1, HALF], F32, f"new1{u}") for u in range(2)]
-        new12 = sbuf([P, 2, HALF], F32, "new12")
-        larger(1, banks1, 0, 1, old0[:, :, cols(1)], new[0])
-        larger(1, banks1, 1, 1, old1[:, :, cols(1)], new[1])
-        scatter(1, 0, new[0][:, 0, :])
-        scatter(1, 1, new[1][:, 0, :])
-        larger(1, banks1, 2, 2, old23[:, :, cols(1)], new12)
-        scatter(1, 2, new12[:, 0, :])
-        scatter(1, 3, new12[:, 1, :])
+        nw1 = [larger(1, u, h1, old) for u, old in enumerate((old0, old1, old2, old3))]
+        for u in range(R):
+            scatter(1, u, nw1[u])
+            nc.sync.dma_start(out=out_rows[:, u, :], in_=page[u][:])

@@ -85,11 +85,11 @@ def tile_picked_tokhopnpagex_none_p_kernel(tc, x_words, x_scales, wa, gt, w1, me
         out_rows = out.rearrange("(p u) w -> p u w", u=R)
 
         nc.vector.memset(x_table_scales[:].bitcast(I32), 0)
-        nc.sync.dma_start(out=wa_raw[:], in_=wa.rearrange("(p t) j -> p t j", t=R))
         nc.sync.dma_start(offs_sb[:], offs)
+        nc.sync.dma_start(out=x_table[:], in_=x_words[0].rearrange("p n t -> p (n t)").bitcast(I32))
         for q in (0, 2, 1, 3):
             nc.sync.dma_start(out=x_table_scales[32 * q : 32 * q + 4, :].bitcast(I32), in_=x_scales[0, 4 * q : 4 * q + 4, :].bitcast(I32))
-        nc.sync.dma_start(out=x_table[:], in_=x_words[0].rearrange("p n t -> p (n t)").bitcast(I32))
+        nc.sync.dma_start(out=wa_raw[:], in_=wa.rearrange("(p t) j -> p t j", t=R))
         nc.sync.dma_start(n1_sb[:], n1)
         nc.sync.dma_start(out=w1_raw[:], in_=w1.rearrange("(p t) m -> p t m", t=R))
         nc.sync.dma_start(n2_sb[:], n2)
@@ -103,11 +103,11 @@ def tile_picked_tokhopnpagex_none_p_kernel(tc, x_words, x_scales, wa, gt, w1, me
         wa_scales = sbuf([P, H], U8, "wa_scales")
         x_codes = sbuf([P, S], U32, "x_codes")
         x_code_scales = sbuf([P, S], U8, "x_code_scales")
+        gather_on_vector(x_codes[:].rearrange("p (t c) -> p c t", t=R), x_table[:].bitcast(U32), offs_sb[:])
+        gather_on_vector(x_code_scales[:].rearrange("p (t c) -> p c t", t=R), x_table_scales[:], offs_sb[:])
         interleave(nc.scalar.copy, wa_bf[:, : WA_ON_SCALAR * R], wa_raw[:, :, :WA_ON_SCALAR])
         interleave(nc.vector.tensor_copy, wa_bf[:, WA_ON_SCALAR * R :], wa_raw[:, :, WA_ON_SCALAR:])
-        gather_on_vector(x_code_scales[:].rearrange("p (t c) -> p c t", t=R), x_table_scales[:], offs_sb[:])
         nc.vector.quantize_mx(out=wa_codes[:].bitcast(FP8X4), scales=wa_scales[:], in_=wa_bf[:])
-        gather_on_vector(x_codes[:].rearrange("p (t c) -> p c t", t=R), x_table[:].bitcast(U32), offs_sb[:])
 
         y_ps = [psum.tile([P, H], F32, name=f"y_ps{t}") for t in range(R)]
         for t in range(R):
@@ -165,8 +165,8 @@ def tile_picked_tokhopnpagex_none_p_kernel(tc, x_words, x_scales, wa, gt, w1, me
             gather(old[:], page[u][:], n3_sb[:])
             return old
 
-        def larger(half, u, h, old, tag=None):
-            nw = sbuf([P, HALF], F32, f"nw{half}_{u}", tag)
+        def larger(half, u, h, old):
+            nw = sbuf([P, HALF], F32, f"nw{half}_{u}")
             nc.vector.scalar_tensor_tensor(out=nw[:], in0=old[:, cols(half)], scalar=0.5, in1=h[u], op0=ALU.mult, op1=ALU.max)
             return nw
 
@@ -177,7 +177,7 @@ def tile_picked_tokhopnpagex_none_p_kernel(tc, x_words, x_scales, wa, gt, w1, me
             0,
             sbuf([P, R, HALF], F32, "st_far0"),
             [gather_on_scalar, gather_on_scalar, gather_on_vector, gather_on_vector],
-            [(slice(0, 2), abs_on_scalar), (slice(2, 3), abs_on_scalar), (slice(3, 4), abs_on_vector)],
+            [(slice(t, t + 1), abs_on_scalar if t < 2 else abs_on_vector) for t in range(R)],
         )
         w1_codes = sbuf([P, N], U32, "w1_codes", "y_far_s")
         w1_scales = sbuf([P, N], U8, "w1_scales")
@@ -202,7 +202,7 @@ def tile_picked_tokhopnpagex_none_p_kernel(tc, x_words, x_scales, wa, gt, w1, me
         old3 = fetch_old(3, gather_on_scalar, "z_bf1")
         scatter(0, 2, larger(0, 2, h0, old2))
         h1 = second_product(1, z_woven1)
-        scatter(0, 3, larger(0, 3, h0, old3, "z_woven1"))
+        scatter(0, 3, larger(0, 3, h0, old3))
 
         nw1 = [larger(1, u, h1, old) for u, old in enumerate((old0, old1, old2, old3))]
         for u in range(R):

from contextlib import ExitStack

import concourse.mybir as mybir

K, T, S, N, H, U = 512, 2048, 512, 512, 512, 1024
FLOPS = 2 * K * S * H + 2 * S * N * H

F32 = mybir.dt.float32
BF16 = mybir.dt.bfloat16
I32 = mybir.dt.int32
U32 = mybir.dt.uint32
U16 = mybir.dt.uint16
U8 = mybir.dt.uint8
FP8X4 = mybir.dt.float8_e4m3fn_x4
ALU = mybir.AluOpType
ACT = mybir.ActivationFunctionType

P = 128
R = 4
HALF = H // 2
LINE = 4
WA_ON_SCALAR = 192
TILES_ON_VECTOR = 2


def tile_picked_tokhopnpagex_none_p_kernel(tc, x_words, x_scales, wa, gt, w1, mem, offs, n1, n2, n3, out):
    nc = tc.nc

    def gather_on_vector(dst, window, offsets):
        nc.vector.tensor_copy(out=dst, in_=window.indirect(offsets))

    def gather_on_scalar(dst, window, offsets):
        nc.scalar.activation(out=dst, in_=window.indirect(offsets), func=ACT.Copy)

    def abs_on_vector(dst, src):
        nc.vector.scalar_tensor_tensor(out=dst, in0=src, scalar=-1.0, in1=src, op0=ALU.mult, op1=ALU.max)

    def abs_on_scalar(dst, src):
        nc.scalar.activation(out=dst, in_=src, func=ACT.Abs)

    def entries(lists, half):
        return lists[:, half * HALF // 16 : (half + 1) * HALF // 16]

    def cols(half):
        return slice(half * HALF, (half + 1) * HALF)

    def interleave(copy, dst, src):
        copy(out=dst.rearrange("p (c i t) -> p c t i", i=LINE, t=R), in_=src.rearrange("p t (c i) -> p c t i", i=LINE))

    def product(dst, lhs_codes, lhs_scales, block, rhs_codes, rhs_scales):
        rows = slice(block * P, (block + 1) * P)
        nc.tensor.matmul_mx(
            out=dst,
            lhsT=lhs_codes[:, rows].bitcast(FP8X4),
            lhsT_scale=lhs_scales[:, rows],
            rhs=rhs_codes[:].bitcast(FP8X4),
            rhs_scale=rhs_scales[:],
            start=True,
            stop=True,
        )

    with ExitStack() as ctx:
        keep = ctx.enter_context(tc.tile_pool(name="keep", bufs=1))
        psum = ctx.enter_context(tc.psum_pool(name="psum", bufs=1))

        def sbuf(shape, dtype, name, tag=None):
            return keep.tile(shape, dtype, name=name, tag=tag or name, align_bytes=64)

        warm_in = sbuf([P, 8], F32, "warm_in")
        warm_out = sbuf([P, 8], F32, "warm_out")
        nc.gpsimd.memset(warm_in[:], 1.0)
        nc.scalar.activation(out=warm_out[:], in_=warm_in[:], func=ACT.Abs_reciprocal_sqrt)

        offs_sb = sbuf([P, S // 16], U16, "offs_sb")
        n1_sb = sbuf([P, H // 16], U16, "n1_sb")
        n2_sb = sbuf([P, H // 16], U16, "n2_sb")
        n3_sb = sbuf([P, H // 16], U16, "n3_sb")
        x_table = sbuf([P, T], I32, "x_table")
        x_table_scales = sbuf([P, T], U8, "x_table_scales")
        gt_sb = sbuf([P, R], F32, "gt_sb")
        wa_raw = sbuf([P, R, H], F32, "wa_raw")
        w1_raw = sbuf([P, R, N], F32, "w1_raw")
        page = [sbuf([P, U], F32, f"page{u}") for u in range(R)]
        mem_rows = mem.rearrange("(p u) w -> p u w", u=R)
        out_rows = out.rearrange("(p u) w -> p u w", u=R)

        nc.vector.memset(x_table_scales[:].bitcast(I32), 0)
        nc.sync.dma_start(offs_sb[:], offs)
        nc.sync.dma_start(out=x_table[:], in_=x_words[0].rearrange("p n t -> p (n t)").bitcast(I32))
        for q in (0, 2, 1, 3):
            nc.sync.dma_start(out=x_table_scales[32 * q : 32 * q + 4, :].bitcast(I32), in_=x_scales[0, 4 * q : 4 * q + 4, :].bitcast(I32))
        nc.sync.dma_start(out=wa_raw[:], in_=wa.rearrange("(p t) j -> p t j", t=R))
        nc.sync.dma_start(n1_sb[:], n1)
        nc.sync.dma_start(out=w1_raw[:], in_=w1.rearrange("(p t) m -> p t m", t=R))
        nc.sync.dma_start(n2_sb[:], n2)
        nc.sync.dma_start(n3_sb[:], n3)
        nc.sync.dma_start(out=gt_sb[:], in_=gt.rearrange("(p t) o -> p (t o)", t=R))
        for u in range(R):
            nc.sync.dma_start(out=page[u][:], in_=mem_rows[:, u, :])

        wa_bf = sbuf([P, H * R], BF16, "wa_bf")
        wa_codes = sbuf([P, H], U32, "wa_codes")
        wa_scales = sbuf([P, H], U8, "wa_scales")
        x_codes = sbuf([P, S], U32, "x_codes")
        x_code_scales = sbuf([P, S], U8, "x_code_scales")
        gather_on_vector(x_codes[:].rearrange("p (t c) -> p c t", t=R), x_table[:].bitcast(U32), offs_sb[:])
        gather_on_vector(x_code_scales[:].rearrange("p (t c) -> p c t", t=R), x_table_scales[:], offs_sb[:])
        interleave(nc.scalar.copy, wa_bf[:, : WA_ON_SCALAR * R], wa_raw[:, :, :WA_ON_SCALAR])
        interleave(nc.vector.tensor_copy, wa_bf[:, WA_ON_SCALAR * R :], wa_raw[:, :, WA_ON_SCALAR:])
        nc.vector.quantize_mx(out=wa_codes[:].bitcast(FP8X4), scales=wa_scales[:], in_=wa_bf[:])

        y_ps = [psum.tile([P, H], F32, name=f"y_ps{t}") for t in range(R)]
        for t in range(R):
            product(y_ps[t][:], x_codes, x_code_scales, t, wa_codes, wa_scales)

        w1_bf = sbuf([P, N * R], BF16, "w1_bf")
        nc.vector.tensor_copy(out=w1_bf[:].rearrange("p (u c t) -> p c u t", u=R, t=R), in_=w1_raw[:].rearrange("p t (c u) -> p c u t", u=R))

        y_sb = [sbuf([P, H], F32, f"y_sb{t}") for t in range(R)]
        y_far_v = sbuf([P, TILES_ON_VECTOR, H], F32, "y_far_v", "w1_raw")
        y_far_s = sbuf([P, R - TILES_ON_VECTOR, H], F32, "y_far_s")
        y_far = [y_far_v[:, 0, :], y_far_v[:, 1, :], y_far_s[:, 0, :], y_far_s[:, 1, :]]
        for t in range(R):
            nc.scalar.copy(out=y_sb[t][:], in_=y_ps[t][:])
        for t in range(R):
            gather = gather_on_vector if t < TILES_ON_VECTOR else gather_on_scalar
            for half in range(2):
                gather(y_far[t][:, cols(half)], y_sb[t][:], entries(n1_sb, half))
        st = [sbuf([P, H], F32, "st0"), sbuf([P, H], F32, "st1"), sbuf([P, H], F32, "st2", "y_sb1"), sbuf([P, H], F32, "st3", "y_sb0")]
        for t in range(R):
            nc.vector.tensor_tensor(out=st[t][:], in0=y_ps[t][:], in1=y_far[t], op=ALU.subtract)

        def reciprocals(half, st_far, gathers, groups):
            size, square, inv = [sbuf([P, R, HALF], F32, f"{name}{half}") for name in ("size", "square", "inv")]
            for t in range(R):
                gathers[t](st_far[:, t, :], st[t][:], entries(n2_sb, half))
            for tiles, absolute in groups:
                absolute(size[:, tiles, :], st_far[:, tiles, :])
                nc.scalar.activation(out=square[:, tiles, :], in_=size[:, tiles, :], func=ACT.Square, bias=0.5)
                nc.scalar.activation(out=inv[:, tiles, :], in_=square[:, tiles, :], func=ACT.Abs_reciprocal_sqrt)
            return inv

        def make_z(half, inv, copy):
            z_bf = sbuf([P, R, HALF], BF16, f"z_bf{half}")
            z_woven = sbuf([P, HALF * R], BF16, f"z_woven{half}")
            for t in range(R):
                nc.vector.scalar_tensor_tensor(
                    out=z_bf[:, t, :], in0=inv[:, t, :], scalar=gt_sb[:, t : t + 1], in1=st[t][:, cols(half)], op0=ALU.mult, op1=ALU.mult
                )
            interleave(copy, z_woven[:], z_bf[:])
            return z_woven

        def second_product(half, z_woven):
            z_codes = sbuf([P, HALF], U32, f"z_codes{half}")
            z_scales = sbuf([P, HALF], U8, f"z_scales{half}")
            nc.vector.quantize_mx(out=z_codes[:].bitcast(FP8X4), scales=z_scales[:], in_=z_woven[:])
            banks = [psum.tile([P, 2, HALF], F32, name=f"h_ps{half}_{b}") for b in range(2)]
            h = [banks[u // 2][:, u % 2, :] for u in range(R)]
            for u in range(R):
                product(h[u], w1_codes, w1_scales, u, z_codes, z_scales)
            return h

        def fetch_old(u, gather, tag):
            old = sbuf([P, H], F32, f"old{u}", tag)
            gather(old[:], page[u][:], n3_sb[:])
            return old

        def larger(half, u, h, old):
            nw = sbuf([P, HALF], F32, f"nw{half}_{u}")
            nc.vector.scalar_tensor_tensor(out=nw[:], in0=old[:, cols(half)], scalar=0.5, in1=h[u], op0=ALU.mult, op1=ALU.max)
            return nw

        def scatter(half, u, nw):
            nc.vector.tensor_copy(out=page[u][:].indirect(entries(n3_sb, half)), in_=nw[:])

        inv0 = reciprocals(
            0,
            sbuf([P, R, HALF], F32, "st_far0"),
            [gather_on_scalar, gather_on_scalar, gather_on_vector, gather_on_vector],
            [(slice(t, t + 1), abs_on_scalar if t < 2 else abs_on_vector) for t in range(R)],
        )
        w1_codes = sbuf([P, N], U32, "w1_codes", "y_far_s")
        w1_scales = sbuf([P, N], U8, "w1_scales")
        nc.vector.quantize_mx(out=w1_codes[:].bitcast(FP8X4), scales=w1_scales[:], in_=w1_bf[:])
        h0 = second_product(0, make_z(0, inv0, nc.vector.tensor_copy))
        old0 = fetch_old(0, gather_on_vector, "z_woven0")
        old1 = fetch_old(1, gather_on_scalar, "square0")

        inv1 = reciprocals(
            1,
            sbuf([P, R, HALF], F32, "st_far1", "size0"),
            [gather_on_scalar] * R,
            [(slice(0, 2), abs_on_scalar), (slice(2, 4), abs_on_scalar)],
        )
        nw01 = larger(0, 1, h0, old1)
        nw00 = larger(0, 0, h0, old0)
        scatter(0, 1, nw01)
        scatter(0, 0, nw00)

        old2 = fetch_old(2, gather_on_scalar, "square1")
        z_woven1 = make_z(1, inv1, nc.scalar.copy)
        old3 = fetch_old(3, gather_on_scalar, "z_bf1")
        scatter(0, 2, larger(0, 2, h0, old2))
        h1 = second_product(1, z_woven1)
        scatter(0, 3, larger(0, 3, h0, old3))

        nw1 = [larger(1, u, h1, old) for u, old in enumerate((old0, old1, old2, old3))]
        for u in range(R):
            scatter(1, u, nw1[u])
            nc.sync.dma_start(out=out_rows[:, u, :], in_=page[u][:])
